import numpy as np
import ml_dtypes


def mxq(x, axis, fmt="e4m3"):
    dtype, down = {"e4m3": (ml_dtypes.float8_e4m3fn, 7), "e5m2": (ml_dtypes.float8_e5m2, 14)}[fmt]
    v = np.moveaxis(np.asarray(x, np.float32).astype(ml_dtypes.bfloat16).astype(np.float64), axis, -1)
    blocks = v.reshape(v.shape[:-1] + (-1, 32))
    amax = np.abs(blocks).max(-1, keepdims=True)
    byte = np.maximum(np.where(amax > 0, np.frexp(amax)[1] - 1 + 127, 0) - down, 1)
    scale = np.exp2(byte - 127.0)
    codes = (blocks / scale).astype(np.float32).astype(dtype).astype(np.float64)
    return np.moveaxis((codes * scale).reshape(v.shape), -1, axis)


WIDE = False


def mx_kscale(k, group=512):
    if not WIDE:
        return np.ones(k)
    levels = np.array([18, -18])
    if group != 512:
        return np.exp2(np.random.permutation(np.resize(levels, k // group))).repeat(group)
    if k % 512:
        return np.exp2(np.random.permutation(np.resize(levels, k // 32))).repeat(32)
    a = np.empty((k // 512, 16))
    for p in range(k // 512):
        a[p, :8] = np.random.permutation(np.resize(levels, 8))
        for g in range(8):
            far = levels[np.abs(levels - a[p, g]) >= 10]
            a[p, g + 8] = far[np.random.randint(len(far))]
    return np.exp2(a.ravel()).repeat(32)


def f64(x):
    return np.asarray(x).astype(np.float64)


E2M1 = np.array([0.0, 0.5, 1.0, 1.5, 2.0, 3.0, 4.0, 6.0, -0.0, -0.5, -1.0, -1.5, -2.0, -3.0, -4.0, -6.0])


def pack_group(w):
    k, n = w.shape
    w = f64(np.asarray(w, np.float32).astype(ml_dtypes.bfloat16)).reshape(k // 32, 32, n)
    amax = np.abs(w).max(1)
    mant, ex = np.frexp(amax / 6.0)
    byte = np.clip(np.where(amax > 0, np.where(mant > 0.5, ex, ex - 1) + 127, 1), 1, 254)
    scaled = (w * np.exp2(127.0 - byte)[:, None, :]).reshape(k, n).astype(np.float32)
    c = np.ascontiguousarray(scaled.reshape(k // 4, 4, n).transpose(0, 2, 1)).astype(ml_dtypes.float4_e2m1fn).view(np.uint8) & 0xF
    return np.ascontiguousarray((c[..., 0::2] | (c[..., 1::2] << 4)).reshape(k // 4, 2 * n)), byte.astype(np.uint8)


def unpack_group(words, scales):
    p, n = words.shape[0], scales.shape[1]
    words = np.ascontiguousarray(words).reshape(p, n, 2)
    nib = np.empty((p, n, 4), np.uint8)
    nib[..., 0::2] = words & 0xF
    nib[..., 1::2] = words >> 4
    return E2M1[nib].transpose(0, 2, 1).reshape(4 * p, n) * np.repeat(np.exp2(scales.astype(np.float64) - 127.0), 32, axis=0)


def gelu(v):
    return 0.5 * v * (1.0 + np.tanh(0.7978845608028654 * (v + 0.044715 * v ** 3)))


G, D, M, N = 4, 128, 256, 512


def setup_inputs():
    n = np.random.standard_normal
    s = mx_kscale(D, 0)[:, None]
    w_ = [pack_group(w) for w in n((G, D, M)) / np.sqrt(D) / s]
    u_ = [pack_group(w) for w in n((G, D, M)) / np.sqrt(D) / s]
    return {
        "x": (n((G, D, N)) * s).astype(np.float32),
        "w_words": np.stack([w[0] for w in w_]),
        "w_scales": np.stack([w[1] for w in w_]),
        "u_words": np.stack([w[0] for w in u_]),
        "u_scales": np.stack([w[1] for w in u_]),
        "r": n((G, M, N)).astype(np.float32),
    }


def reference(x, w_words, w_scales, u_words, u_scales, r):
    xq = mxq(f64(x), 1, "e4m3")
    h = np.stack([unpack_group(w_words[g], w_scales[g]) for g in range(G)]).transpose(0, 2, 1) @ xq
    g = np.stack([unpack_group(u_words[g], u_scales[g]) for g in range(G)]).transpose(0, 2, 1) @ xq
    y = gelu(h) * g
    y = y + f64(r)
    return y

@@ -1,0 +1,151 @@
+from contextlib import ExitStack
+
+import concourse.mybir as mybir
+
+G, D, M, N = 4, 128, 256, 512
+FLOPS = 2 * 2 * G * D * M * N
+
+F32 = mybir.dt.float32
+BF16 = mybir.dt.bfloat16
+U32 = mybir.dt.uint32
+I32 = mybir.dt.int32
+U8 = mybir.dt.uint8
+FP8X4 = mybir.dt.float8_e4m3fn_x4
+FP4X4 = mybir.dt.float4_e2m1fn_x4
+GELU = mybir.ActivationFunctionType.Gelu_apprx_tanh
+ADD = mybir.AluOpType.add
+MULT = mybir.AluOpType.mult
+
+P = 128
+PACK = 4
+ROWS = D // PACK
+SCALE_ROWS = D // 32
+HALVES = M // P
+X_CHUNKS = [256,256]
+SCALAR_COLS = [80,80]
+GPSIMD_COLS = [224,224,224,224,224,224,224,0]
+TILES = [(0, 0), (1, 0), (0, 1), (1, 1), (2, 0), (3, 0), (2, 1), (3, 1)]
+
+
+def tile_rows_gglu_gelu_res_kernel(tc, x, w_words, w_scales, u_words, u_scales, r, out):
+    nc = tc.nc
+    with ExitStack() as ctx:
+        sb = ctx.enter_context(tc.tile_pool(name="sb", bufs=1))
+        ps = ctx.enter_context(tc.psum_pool(name="ps", bufs=1))
+        ctx.enter_context(tc.manual_schedule())
+
+        words = [sb.tile([P, 2 * M], U8, name="words%d" % i, align_bytes=64) for i in range(2)]
+        scales = sb.tile([P, 2, M], U8, name="scales", align_bytes=64)
+        x_codes = sb.tile([P, N], U32, name="x_codes", align_bytes=64)
+        x_scales = sb.tile([P, N], U8, name="x_scales", align_bytes=64)
+        x_bf = sb.tile([P, N, PACK], BF16, name="x_bf", align_bytes=64)
+        zero = sb.tile([P, 1], F32, name="zero")
+        bias = sb.tile([P, 1], F32, name="bias")
+        banks = [[ps.tile([P, N], F32, name="bank%d_%d" % (g, i)) for i in range(2)] for g in range(G)]
+        res = [sb.tile([P, 2, N], F32, name="res%d" % i) for i in range(len(TILES) // 2)]
+        act = [sb.tile([P, N], F32, name="act%d" % i) for i in range(len(TILES))]
+        prod = [sb.tile([P, N], F32, name="prod%d" % i) for i in range(len(TILES))]
+        y = [sb.tile([P, N], F32, name="y%d" % i) for i in range(len(TILES))]
+
+        nc.vector.memset(scales[:].rearrange("p i m -> p (i m)").bitcast(I32), 0)
+        nc.gpsimd.memset(zero[:], 0.0)
+        nc.scalar.activation(out=bias[:], in_=zero[:], func=GELU)
+
+        x_view = x.rearrange("g (p j) n -> (g p) j n", j=PACK)
+        x_raw = []
+        c0 = 0
+        for i, width in enumerate(X_CHUNKS):
+            raw = sb.tile([P, PACK, width], F32, name="x_raw%d" % i)
+            nc.sync.dma_start(out=raw[:], in_=x_view[:, :, c0 : c0 + width])
+            x_raw.append((raw, c0, width))
+            c0 += width
+
+        def load_words(i):
+            src = (w_words, u_words)[i].rearrange("g p b -> (g p) b")
+            nc.sync.dma_start(out=words[i][:].bitcast(I32), in_=src.bitcast(I32))
+
+        def load_scales(g, i):
+            src = (w_scales, u_scales)[i][g]
+            nc.sync.dma_start(out=scales[ROWS * g : ROWS * g + SCALE_ROWS, i, :].bitcast(I32), in_=src.bitcast(I32))
+
+        def load_res(k):
+            g, h = TILES[2 * k]
+            src = r[g : g + 2, h * P : (h + 1) * P, :].rearrange("g p n -> p g n")
+            nc.sync.dma_start(out=res[k][:], in_=src)
+
+        load_words(0)
+        load_scales(0, 0)
+        load_scales(1, 0)
+        load_words(1)
+        load_scales(0, 1)
+        load_scales(1, 1)
+        load_res(0)
+        for g in (2, 3):
+            load_scales(g, 0)
+            load_scales(g, 1)
+        for k in (1, 2, 3):
+            load_res(k)
+
+
+        def interleave(engine_copy, raw, c0, lo, hi):
+            engine_copy(
+                out=x_bf[:, c0 + lo : c0 + hi, :].rearrange("p (c i) t -> p c t i", i=4),
+                in_=raw[:, :, lo:hi].rearrange("p t (c i) -> p c t i", i=4),
+            )
+
+        for (raw, c0, width), scalar_cols in zip(x_raw, SCALAR_COLS):
+            interleave(nc.vector.tensor_copy, raw, c0, 0, width - scalar_cols)
+            if scalar_cols:
+                interleave(nc.scalar.copy, raw, c0, width - scalar_cols, width)
+            nc.vector.quantize_mx(
+                out=x_codes[:, c0 : c0 + width].bitcast(FP8X4),
+                scales=x_scales[:, c0 : c0 + width],
+                in_=x_bf[:, c0 : c0 + width, :].rearrange("p c t -> p (c t)"),
+            )
+
+        def product(t, i):
+            g, h = TILES[t]
+            rows = slice(ROWS * g, ROWS * (g + 1))
+            nc.tensor.matmul_mx(
+                out=banks[g][i][:],
+                lhsT=words[i][rows, 2 * P * h : 2 * P * (h + 1)].bitcast(FP4X4),
+                lhsT_scale=scales[rows, i, P * h : P * (h + 1)],
+                rhs=x_codes[rows, :].bitcast(FP8X4),
+                rhs_scale=x_scales[rows, :],
+                start=True,
+                stop=True,
+            )
+
+        def products(k):
+            for i in range(2):
+                for t in (2 * k, 2 * k + 1):
+                    product(t, i)
+
+        def gate(t):
+            g = TILES[t][0]
+            nc.scalar.activation(out=act[t][:], in_=banks[g][0][:], func=GELU, bias=bias[:])
+            nc.vector.tensor_tensor(out=prod[t][:], in0=banks[g][1][:], in1=act[t][:], op=MULT)
+
+        def add(engine, t, lo, hi):
+            if hi > lo:
+                engine.tensor_tensor(out=y[t][:, lo:hi], in0=prod[t][:, lo:hi], in1=res[t // 2][:, t % 2, lo:hi], op=ADD)
+
+        def store(t):
+            g, h = TILES[t]
+            nc.sync.dma_start(out=out[g, h * P : (h + 1) * P, :], in_=y[t][:])
+
+        last = len(TILES) - 1
+        products(0)
+        for t in range(len(TILES)):
+            gate(t)
+            if t == 1:
+                products(1)
+                products(2)
+            if t == 5:
+                products(3)
+            add(nc.gpsimd, t, 0, GPSIMD_COLS[t])
+            if t > 0:
+                add(nc.vector, t - 1, GPSIMD_COLS[t - 1], N)
+                store(t - 1)
+        add(nc.vector, last, GPSIMD_COLS[last], N)
+        store(last)

@@ -23,8 +23,7 @@ SCALE_ROWS = D // 32
 HALVES = M // P
 X_CHUNKS = [256,256]
 SCALAR_COLS = [80,80]
-GPSIMD_COLS = [224,224,224,224,224,224,224,0]
-TILES = [(0, 0), (1, 0), (0, 1), (1, 1), (2, 0), (3, 0), (2, 1), (3, 1)]
+TILES = [(0, 0), (1, 0), (2, 0), (3, 0), (0, 1), (1, 1), (2, 1), (3, 1)]
 
 
 def tile_rows_gglu_gelu_res_kernel(tc, x, w_words, w_scales, u_words, u_scales, r, out):
@@ -49,6 +48,22 @@ def tile_rows_gglu_gelu_res_kernel(tc, x, w_words, w_scales, u_words, u_scales, 
 
         nc.vector.memset(scales[:].rearrange("p i m -> p (i m)").bitcast(I32), 0)
         nc.gpsimd.memset(zero[:], 0.0)
+
+        def load_words(i):
+            src = (w_words, u_words)[i].rearrange("g p b -> (g p) b")
+            nc.sync.dma_start(out=words[i][:].bitcast(I32), in_=src.bitcast(I32))
+
+        def load_scales(queue, g, i):
+            src = (w_scales, u_scales)[i][g]
+            queue.dma_start(out=scales[ROWS * g : ROWS * g + SCALE_ROWS, i, :].bitcast(I32), in_=src.bitcast(I32))
+
+        def load_res(k):
+            g, h = TILES[2 * k]
+            src = r[g : g + 2, h * P : (h + 1) * P, :].rearrange("g p n -> p g n")
+            nc.sync.dma_start(out=res[k][:], in_=src)
+
+        for g in range(G):
+            load_scales(nc.scalar, g, 0)
         nc.scalar.activation(out=bias[:], in_=zero[:], func=GELU)
 
         x_view = x.rearrange("g (p j) n -> (g p) j n", j=PACK)
@@ -60,30 +75,11 @@ def tile_rows_gglu_gelu_res_kernel(tc, x, w_words, w_scales, u_words, u_scales, 
             x_raw.append((raw, c0, width))
             c0 += width
 
-        def load_words(i):
-            src = (w_words, u_words)[i].rearrange("g p b -> (g p) b")
-            nc.sync.dma_start(out=words[i][:].bitcast(I32), in_=src.bitcast(I32))
-
-        def load_scales(g, i):
-            src = (w_scales, u_scales)[i][g]
-            nc.sync.dma_start(out=scales[ROWS * g : ROWS * g + SCALE_ROWS, i, :].bitcast(I32), in_=src.bitcast(I32))
-
-        def load_res(k):
-            g, h = TILES[2 * k]
-            src = r[g : g + 2, h * P : (h + 1) * P, :].rearrange("g p n -> p g n")
-            nc.sync.dma_start(out=res[k][:], in_=src)
-
         load_words(0)
-        load_scales(0, 0)
-        load_scales(1, 0)
         load_words(1)
-        load_scales(0, 1)
-        load_scales(1, 1)
-        load_res(0)
-        for g in (2, 3):
-            load_scales(g, 0)
-            load_scales(g, 1)
-        for k in (1, 2, 3):
+        for g in range(G):
+            load_scales(nc.sync, g, 1)
+        for k in range(4):
             load_res(k)
 
 
@@ -116,36 +112,35 @@ def tile_rows_gglu_gelu_res_kernel(tc, x, w_words, w_scales, u_words, u_scales, 
                 stop=True,
             )
 
-        def products(k):
-            for i in range(2):
-                for t in (2 * k, 2 * k + 1):
-                    product(t, i)
-
-        def gate(t):
+        def gate(t, lo, hi):
             g = TILES[t][0]
-            nc.scalar.activation(out=act[t][:], in_=banks[g][0][:], func=GELU, bias=bias[:])
-            nc.vector.tensor_tensor(out=prod[t][:], in0=banks[g][1][:], in1=act[t][:], op=MULT)
+            nc.scalar.activation(out=act[t][:, lo:hi], in_=banks[g][0][:, lo:hi], func=GELU, bias=bias[:])
+            nc.vector.tensor_tensor(out=prod[t][:, lo:hi], in0=banks[g][1][:, lo:hi], in1=act[t][:, lo:hi], op=MULT)
 
         def add(engine, t, lo, hi):
             if hi > lo:
                 engine.tensor_tensor(out=y[t][:, lo:hi], in0=prod[t][:, lo:hi], in1=res[t // 2][:, t % 2, lo:hi], op=ADD)
 
-        def store(t):
+        def store(t, lo, hi):
             g, h = TILES[t]
-            nc.sync.dma_start(out=out[g, h * P : (h + 1) * P, :], in_=y[t][:])
+            nc.sync.dma_start(out=out[g, h * P : (h + 1) * P, lo:hi], in_=y[t][:, lo:hi])
 
-        last = len(TILES) - 1
-        products(0)
+        for i in range(2):
+            for t in range(G):
+                product(t, i)
         for t in range(len(TILES)):
-            gate(t)
-            if t == 1:
-                products(1)
-                products(2)
-            if t == 5:
-                products(3)
-            add(nc.gpsimd, t, 0, GPSIMD_COLS[t])
-            if t > 0:
-                add(nc.vector, t - 1, GPSIMD_COLS[t - 1], N)
-                store(t - 1)
-        add(nc.vector, last, GPSIMD_COLS[last], N)
-        store(last)
+            gate(t, 0, N)
+            if t < G:
+                product(t + G, 0)
+            if 0 < t < G:
+                product(t + G - 1, 1)
+            if t == G - 1:
+                product(t + G, 1)
+            if t < 3:
+                add(nc.gpsimd, t, 0, N)
+                store(t, 0, N)
+        for t in range(3, len(TILES)):
+            cuts = [0, N // 2, N] if t in (3, 7) else [0, N]
+            for lo, hi in zip(cuts, cuts[1:]):
+                add(nc.vector, t, lo, hi)
+                store(t, lo, hi)

@@ -20,10 +20,10 @@ P = 128
 PACK = 4
 ROWS = D // PACK
 SCALE_ROWS = D // 32
-HALVES = M // P
-X_CHUNKS = [256,256]
-SCALAR_COLS = [80,80]
-TILES = [(0, 0), (1, 0), (2, 0), (3, 0), (0, 1), (1, 1), (2, 1), (3, 1)]
+HALF = N // 2
+SCALAR_COLS = 80
+GPSIMD_COLS = 416
+TILES = [(g, h) for h in range(M // P) for g in range(G)]
 
 
 def tile_rows_gglu_gelu_res_kernel(tc, x, w_words, w_scales, u_words, u_scales, r, out):
@@ -35,19 +35,27 @@ def tile_rows_gglu_gelu_res_kernel(tc, x, w_words, w_scales, u_words, u_scales, 
 
         words = [sb.tile([P, 2 * M], U8, name="words%d" % i, align_bytes=64) for i in range(2)]
         scales = sb.tile([P, 2, M], U8, name="scales", align_bytes=64)
-        x_codes = sb.tile([P, N], U32, name="x_codes", align_bytes=64)
-        x_scales = sb.tile([P, N], U8, name="x_scales", align_bytes=64)
+        x_codes = sb.tile([P, HALF + N], U32, name="x_codes", align_bytes=64)
+        x_scales = sb.tile([P, HALF + N], U8, name="x_scales", align_bytes=64)
         x_bf = sb.tile([P, N, PACK], BF16, name="x_bf", align_bytes=64)
+        x_raw = [sb.tile([P, PACK, HALF], F32, name="x_raw%d" % i) for i in range(2)]
         zero = sb.tile([P, 1], F32, name="zero")
         bias = sb.tile([P, 1], F32, name="bias")
         banks = [[ps.tile([P, N], F32, name="bank%d_%d" % (g, i)) for i in range(2)] for g in range(G)]
-        res = [sb.tile([P, 2, N], F32, name="res%d" % i) for i in range(len(TILES) // 2)]
-        act = [sb.tile([P, N], F32, name="act%d" % i) for i in range(len(TILES))]
-        prod = [sb.tile([P, N], F32, name="prod%d" % i) for i in range(len(TILES))]
-        y = [sb.tile([P, N], F32, name="y%d" % i) for i in range(len(TILES))]
+        res = sb.tile([P, len(TILES), N], F32, name="res")
+        act = sb.tile([P, len(TILES), N], F32, name="act")
+        prod = sb.tile([P, len(TILES), N], F32, name="prod")
+        y = sb.tile([P, len(TILES), N], F32, name="y")
 
         nc.vector.memset(scales[:].rearrange("p i m -> p (i m)").bitcast(I32), 0)
+        nc.vector.memset(x_codes[:, 0:HALF], 0)
+        nc.vector.memset(x_scales[:, 0:HALF].bitcast(I32), 0)
         nc.gpsimd.memset(zero[:], 0.0)
+
+        x_view = x.rearrange("g (p j) n -> (g p) j n", j=PACK)
+
+        def load_x(c):
+            nc.sync.dma_start(out=x_raw[c][:], in_=x_view[:, :, c * HALF : (c + 1) * HALF])
 
         def load_words(i):
             src = (w_words, u_words)[i].rearrange("g p b -> (g p) b")
@@ -57,90 +65,100 @@ def tile_rows_gglu_gelu_res_kernel(tc, x, w_words, w_scales, u_words, u_scales, 
             src = (w_scales, u_scales)[i][g]
             queue.dma_start(out=scales[ROWS * g : ROWS * g + SCALE_ROWS, i, :].bitcast(I32), in_=src.bitcast(I32))
 
-        def load_res(k):
-            g, h = TILES[2 * k]
-            src = r[g : g + 2, h * P : (h + 1) * P, :].rearrange("g p n -> p g n")
-            nc.sync.dma_start(out=res[k][:], in_=src)
+        def load_res(t, count):
+            g, h = TILES[t]
+            src = r[g : g + count, h * P : (h + 1) * P, :].rearrange("g p n -> p g n")
+            nc.sync.dma_start(out=res[:, t : t + count, :], in_=src)
 
-        for g in range(G):
-            load_scales(nc.scalar, g, 0)
         nc.scalar.activation(out=bias[:], in_=zero[:], func=GELU)
-
-        x_view = x.rearrange("g (p j) n -> (g p) j n", j=PACK)
-        x_raw = []
-        c0 = 0
-        for i, width in enumerate(X_CHUNKS):
-            raw = sb.tile([P, PACK, width], F32, name="x_raw%d" % i)
-            nc.sync.dma_start(out=raw[:], in_=x_view[:, :, c0 : c0 + width])
-            x_raw.append((raw, c0, width))
-            c0 += width
-
+        load_x(0)
+        for g in range(G):
+            load_scales(nc.sync, g, 0)
+        for g in (0, 1):
+            load_scales(nc.gpsimd, g, 1)
         load_words(0)
         load_words(1)
-        for g in range(G):
+        load_x(1)
+        for g in (2, 3):
             load_scales(nc.sync, g, 1)
-        for k in range(4):
-            load_res(k)
+        for t, count in ((0, 1), (1, 1), (2, 2), (4, 2), (6, 2)):
+            load_res(t, count)
 
-
-        def interleave(engine_copy, raw, c0, lo, hi):
+        def interleave(engine_copy, c, lo, hi):
             engine_copy(
-                out=x_bf[:, c0 + lo : c0 + hi, :].rearrange("p (c i) t -> p c t i", i=4),
-                in_=raw[:, :, lo:hi].rearrange("p t (c i) -> p c t i", i=4),
+                out=x_bf[:, c * HALF + lo : c * HALF + hi, :].rearrange("p (c i) t -> p c t i", i=4),
+                in_=x_raw[c][:, :, lo:hi].rearrange("p t (c i) -> p c t i", i=4),
             )
 
-        for (raw, c0, width), scalar_cols in zip(x_raw, SCALAR_COLS):
-            interleave(nc.vector.tensor_copy, raw, c0, 0, width - scalar_cols)
-            if scalar_cols:
-                interleave(nc.scalar.copy, raw, c0, width - scalar_cols, width)
+        for c in range(2):
+            interleave(nc.vector.tensor_copy, c, 0, HALF - SCALAR_COLS)
+            interleave(nc.scalar.copy, c, HALF - SCALAR_COLS, HALF)
+            cols = slice((c + 1) * HALF, (c + 2) * HALF)
             nc.vector.quantize_mx(
-                out=x_codes[:, c0 : c0 + width].bitcast(FP8X4),
-                scales=x_scales[:, c0 : c0 + width],
-                in_=x_bf[:, c0 : c0 + width, :].rearrange("p c t -> p (c t)"),
+                out=x_codes[:, cols].bitcast(FP8X4),
+                scales=x_scales[:, cols],
+                in_=x_bf[:, c * HALF : (c + 1) * HALF, :].rearrange("p c t -> p (c t)"),
             )
 
-        def product(t, i):
+        def product(t, i, first):
             g, h = TILES[t]
             rows = slice(ROWS * g, ROWS * (g + 1))
             nc.tensor.matmul_mx(
                 out=banks[g][i][:],
                 lhsT=words[i][rows, 2 * P * h : 2 * P * (h + 1)].bitcast(FP4X4),
                 lhsT_scale=scales[rows, i, P * h : P * (h + 1)],
-                rhs=x_codes[rows, :].bitcast(FP8X4),
-                rhs_scale=x_scales[rows, :],
+                rhs=x_codes[rows, first : first + N].bitcast(FP8X4),
+                rhs_scale=x_scales[rows, first : first + N],
                 start=True,
                 stop=True,
             )
 
         def gate(t, lo, hi):
             g = TILES[t][0]
-            nc.scalar.activation(out=act[t][:, lo:hi], in_=banks[g][0][:, lo:hi], func=GELU, bias=bias[:])
-            nc.vector.tensor_tensor(out=prod[t][:, lo:hi], in0=banks[g][1][:, lo:hi], in1=act[t][:, lo:hi], op=MULT)
+            src = slice(N - (hi - lo), N)
+            nc.scalar.activation(out=act[:, t, lo:hi], in_=banks[g][0][:, src], func=GELU, bias=bias[:])
+            nc.vector.tensor_tensor(out=prod[:, t, lo:hi], in0=banks[g][1][:, src], in1=act[:, t, lo:hi], op=MULT)
 
-        def add(engine, t, lo, hi):
-            if hi > lo:
-                engine.tensor_tensor(out=y[t][:, lo:hi], in0=prod[t][:, lo:hi], in1=res[t // 2][:, t % 2, lo:hi], op=ADD)
+        def add(engine, t, count, lo, hi):
+            where = (slice(0, P), slice(t, t + count), slice(lo, hi))
+            engine.tensor_tensor(out=y[where], in0=prod[where], in1=res[where], op=ADD)
 
-        def store(t, lo, hi):
+        def store(t):
             g, h = TILES[t]
-            nc.sync.dma_start(out=out[g, h * P : (h + 1) * P, lo:hi], in_=y[t][:, lo:hi])
+            nc.sync.dma_start(out=out[g, h * P : (h + 1) * P, :], in_=y[:, t, :])
+
+        def refill(g, shift):
+            product(g + shift, 0, HALF)
+            if g > 0:
+                product(g - 1 + shift, 1, HALF)
+            if g == G - 1:
+                product(g + shift, 1, HALF)
 
         for i in range(2):
-            for t in range(G):
-                product(t, i)
-        for t in range(len(TILES)):
-            gate(t, 0, N)
-            if t < G:
-                product(t + G, 0)
-            if 0 < t < G:
-                product(t + G - 1, 1)
-            if t == G - 1:
-                product(t + G, 1)
-            if t < 3:
-                add(nc.gpsimd, t, 0, N)
-                store(t, 0, N)
-        for t in range(3, len(TILES)):
-            cuts = [0, N // 2, N] if t in (3, 7) else [0, N]
-            for lo, hi in zip(cuts, cuts[1:]):
-                add(nc.vector, t, lo, hi)
-                store(t, lo, hi)
+            for g in range(G):
+                product(g, i, 0)
+        for g in range(G):
+            gate(g, 0, HALF)
+            refill(g, 0)
+            if g < 2:
+                add(nc.gpsimd, g, 1, 0, HALF)
+        for g in range(G):
+            gate(g, HALF, N)
+            refill(g, G)
+            if g == 1:
+                add(nc.gpsimd, 0, 2, HALF, N)
+                store(0)
+                store(1)
+        gate(4, 0, N)
+        gate(5, 0, N)
+        add(nc.vector, 2, 2, 0, N)
+        store(2)
+        store(3)
+        add(nc.gpsimd, 5, 1, 0, GPSIMD_COLS)
+        gate(6, 0, N)
+        gate(7, 0, N)
+        add(nc.vector, 5, 1, GPSIMD_COLS, N)
+        store(5)
+        for t in (4, 6, 7):
+            add(nc.vector, t, 1, 0, N)
+            store(t)

@@ -74,15 +74,14 @@ def tile_rows_gglu_gelu_res_kernel(tc, x, w_words, w_scales, u_words, u_scales, 
         load_x(0)
         for g in range(G):
             load_scales(nc.sync, g, 0)
-        for g in (0, 1):
-            load_scales(nc.gpsimd, g, 1)
+        load_scales(nc.gpsimd, 0, 1)
         load_words(0)
-        load_words(1)
         load_x(1)
-        for g in (2, 3):
+        load_words(1)
+        for g in range(1, G):
             load_scales(nc.sync, g, 1)
-        for t, count in ((0, 1), (1, 1), (2, 2), (4, 2), (6, 2)):
-            load_res(t, count)
+        for t in range(0, len(TILES), 2):
+            load_res(t, 2)
 
         def interleave(engine_copy, c, lo, hi):
             engine_copy(
@@ -140,25 +139,25 @@ def tile_rows_gglu_gelu_res_kernel(tc, x, w_words, w_scales, u_words, u_scales, 
         for g in range(G):
             gate(g, 0, HALF)
             refill(g, 0)
-            if g < 2:
-                add(nc.gpsimd, g, 1, 0, HALF)
+            if g == 1:
+                add(nc.gpsimd, 0, 2, 0, HALF)
         for g in range(G):
             gate(g, HALF, N)
             refill(g, G)
-            if g == 1:
-                add(nc.gpsimd, 0, 2, HALF, N)
+            if g == 0:
+                add(nc.gpsimd, 0, 1, HALF, N)
                 store(0)
-                store(1)
-        gate(4, 0, N)
-        gate(5, 0, N)
-        add(nc.vector, 2, 2, 0, N)
+        add(nc.vector, 1, 1, HALF, N)
+        store(1)
+        add(nc.vector, 2, 1, 0, N)
         store(2)
-        store(3)
-        add(nc.gpsimd, 5, 1, 0, GPSIMD_COLS)
-        gate(6, 0, N)
-        gate(7, 0, N)
-        add(nc.vector, 5, 1, GPSIMD_COLS, N)
-        store(5)
-        for t in (4, 6, 7):
+        for t in (4, 6):
+            add(nc.gpsimd, t - 1, 1, 0, GPSIMD_COLS)
+            gate(t, 0, N)
+            gate(t + 1, 0, N)
+            add(nc.vector, t - 1, 1, GPSIMD_COLS, N)
+            store(t - 1)
             add(nc.vector, t, 1, 0, N)
             store(t)
+        add(nc.vector, 7, 1, 0, N)
+        store(7)

@@ -122,6 +122,10 @@ def tile_rows_gglu_gelu_res_kernel(tc, x, w_words, w_scales, u_words, u_scales, 
             where = (slice(0, P), slice(t, t + count), slice(lo, hi))
             engine.tensor_tensor(out=y[where], in0=prod[where], in1=res[where], op=ADD)
 
+        def add_run(lo, hi):
+            flat = [tile[:].rearrange("p t n -> p (t n)")[:, lo:hi] for tile in (y, prod, res)]
+            nc.vector.tensor_tensor(out=flat[0], in0=flat[1], in1=flat[2], op=ADD)
+
         def store(t):
             g, h = TILES[t]
             nc.sync.dma_start(out=out[g, h * P : (h + 1) * P, :], in_=y[:, t, :])
@@ -147,17 +151,20 @@ def tile_rows_gglu_gelu_res_kernel(tc, x, w_words, w_scales, u_words, u_scales, 
             if g == 0:
                 add(nc.gpsimd, 0, 1, HALF, N)
                 store(0)
-        add(nc.vector, 1, 1, HALF, N)
+        add_run(N + HALF, 3 * N)
         store(1)
-        add(nc.vector, 2, 1, 0, N)
         store(2)
-        for t in (4, 6):
-            add(nc.gpsimd, t - 1, 1, 0, GPSIMD_COLS)
-            gate(t, 0, N)
-            gate(t + 1, 0, N)
-            add(nc.vector, t - 1, 1, GPSIMD_COLS, N)
-            store(t - 1)
+        add(nc.gpsimd, 3, 1, 0, GPSIMD_COLS)
+        gate(4, 0, N)
+        gate(5, 0, N)
+        add_run(3 * N + GPSIMD_COLS, 5 * N)
+        store(3)
+        store(4)
+        add(nc.gpsimd, 5, 1, 0, GPSIMD_COLS)
+        gate(6, 0, N)
+        gate(7, 0, N)
+        add(nc.vector, 5, 1, GPSIMD_COLS, N)
+        store(5)
+        for t in (6, 7):
             add(nc.vector, t, 1, 0, N)
             store(t)
-        add(nc.vector, 7, 1, 0, N)
-        store(7)

@@ -65,10 +65,10 @@ def tile_rows_gglu_gelu_res_kernel(tc, x, w_words, w_scales, u_words, u_scales, 
             src = (w_scales, u_scales)[i][g]
             queue.dma_start(out=scales[ROWS * g : ROWS * g + SCALE_ROWS, i, :].bitcast(I32), in_=src.bitcast(I32))
 
-        def load_res(t, count):
+        def load_res(t, count, lo, hi):
             g, h = TILES[t]
-            src = r[g : g + count, h * P : (h + 1) * P, :].rearrange("g p n -> p g n")
-            nc.sync.dma_start(out=res[:, t : t + count, :], in_=src)
+            src = r[g : g + count, h * P : (h + 1) * P, lo:hi].rearrange("g p n -> p g n")
+            nc.sync.dma_start(out=res[:, t : t + count, lo:hi], in_=src)
 
         nc.scalar.activation(out=bias[:], in_=zero[:], func=GELU)
         load_x(0)
@@ -80,8 +80,11 @@ def tile_rows_gglu_gelu_res_kernel(tc, x, w_words, w_scales, u_words, u_scales, 
         load_words(1)
         for g in range(1, G):
             load_scales(nc.sync, g, 1)
-        for t in range(0, len(TILES), 2):
-            load_res(t, 2)
+        load_res(0, 2, 0, HALF)
+        load_res(2, 2, 0, HALF)
+        load_res(0, G, HALF, N)
+        load_res(4, 2, 0, N)
+        load_res(6, 2, 0, N)
 
         def interleave(engine_copy, c, lo, hi):
             engine_copy(
@@ -89,15 +92,19 @@ def tile_rows_gglu_gelu_res_kernel(tc, x, w_words, w_scales, u_words, u_scales, 
                 in_=x_raw[c][:, :, lo:hi].rearrange("p t (c i) -> p c t i", i=4),
             )
 
-        for c in range(2):
-            interleave(nc.vector.tensor_copy, c, 0, HALF - SCALAR_COLS)
-            interleave(nc.scalar.copy, c, HALF - SCALAR_COLS, HALF)
-            cols = slice((c + 1) * HALF, (c + 2) * HALF)
+        def quantize(lo, hi):
             nc.vector.quantize_mx(
-                out=x_codes[:, cols].bitcast(FP8X4),
-                scales=x_scales[:, cols],
-                in_=x_bf[:, c * HALF : (c + 1) * HALF, :].rearrange("p c t -> p (c t)"),
+                out=x_codes[:, HALF + lo : HALF + hi].bitcast(FP8X4),
+                scales=x_scales[:, HALF + lo : HALF + hi],
+                in_=x_bf[:, lo:hi, :].rearrange("p c t -> p (c t)"),
             )
+
+        for c in range(2):
+            interleave(nc.vector.tensor_copy, c, 0, P)
+            interleave(nc.vector.tensor_copy, c, P, HALF - SCALAR_COLS)
+            interleave(nc.scalar.copy, c, HALF - SCALAR_COLS, HALF)
+            quantize(c * HALF, c * HALF + P)
+            quantize(c * HALF + P, (c + 1) * HALF)
 
         def product(t, i, first):
             g, h = TILES[t]
@@ -112,23 +119,26 @@ def tile_rows_gglu_gelu_res_kernel(tc, x, w_words, w_scales, u_words, u_scales, 
                 stop=True,
             )
 
+        def gelu(t, lo, hi, at):
+            bank = banks[TILES[t][0]][0]
+            nc.scalar.activation(out=act[:, t, lo:hi], in_=bank[:, at : at + hi - lo], func=GELU, bias=bias[:])
+
+        def multiply(t, lo, hi, at):
+            bank = banks[TILES[t][0]][1]
+            nc.vector.tensor_tensor(out=prod[:, t, lo:hi], in0=bank[:, at : at + hi - lo], in1=act[:, t, lo:hi], op=MULT)
+
         def gate(t, lo, hi):
-            g = TILES[t][0]
-            src = slice(N - (hi - lo), N)
-            nc.scalar.activation(out=act[:, t, lo:hi], in_=banks[g][0][:, src], func=GELU, bias=bias[:])
-            nc.vector.tensor_tensor(out=prod[:, t, lo:hi], in0=banks[g][1][:, src], in1=act[:, t, lo:hi], op=MULT)
+            gelu(t, lo, hi, N - (hi - lo))
+            multiply(t, lo, hi, N - (hi - lo))
 
         def add(engine, t, count, lo, hi):
             where = (slice(0, P), slice(t, t + count), slice(lo, hi))
             engine.tensor_tensor(out=y[where], in0=prod[where], in1=res[where], op=ADD)
 
-        def add_run(lo, hi):
-            flat = [tile[:].rearrange("p t n -> p (t n)")[:, lo:hi] for tile in (y, prod, res)]
-            nc.vector.tensor_tensor(out=flat[0], in0=flat[1], in1=flat[2], op=ADD)
-
-        def store(t):
+        def store(t, count=1, lo=0, hi=N):
             g, h = TILES[t]
-            nc.sync.dma_start(out=out[g, h * P : (h + 1) * P, :], in_=y[:, t, :])
+            dst = out[g : g + count, h * P : (h + 1) * P, lo:hi].rearrange("g p n -> p g n")
+            nc.sync.dma_start(out=dst, in_=y[:, t : t + count, lo:hi])
 
         def refill(g, shift):
             product(g + shift, 0, HALF)
@@ -143,22 +153,22 @@ def tile_rows_gglu_gelu_res_kernel(tc, x, w_words, w_scales, u_words, u_scales, 
         for g in range(G):
             gate(g, 0, HALF)
             refill(g, 0)
-            if g == 1:
-                add(nc.gpsimd, 0, 2, 0, HALF)
+            if g == 0:
+                add(nc.gpsimd, 0, 1, 0, HALF)
+        add(nc.vector, 1, 1, 0, HALF)
+        store(0, 2, 0, HALF)
+        add(nc.gpsimd, 2, 2, 0, HALF)
+        store(2, 2, 0, HALF)
         for g in range(G):
             gate(g, HALF, N)
             refill(g, G)
-            if g == 0:
-                add(nc.gpsimd, 0, 1, HALF, N)
-                store(0)
-        add_run(N + HALF, 3 * N)
-        store(1)
-        store(2)
-        add(nc.gpsimd, 3, 1, 0, GPSIMD_COLS)
+        add(nc.vector, 0, 2, HALF, N)
+        store(0, 2, HALF, N)
+        add(nc.gpsimd, 2, 2, HALF, N)
+        store(2, 2, HALF, N)
         gate(4, 0, N)
         gate(5, 0, N)
-        add_run(3 * N + GPSIMD_COLS, 5 * N)
-        store(3)
+        add(nc.vector, 4, 1, 0, N)
         store(4)
         add(nc.gpsimd, 5, 1, 0, GPSIMD_COLS)
         gate(6, 0, N)

@@ -21,9 +21,12 @@ PACK = 4
 ROWS = D // PACK
 SCALE_ROWS = D // 32
 HALF = N // 2
+RUN = 4
+W, U = 0, 1
+ROUNDS = [(0, 0, HALF), (0, HALF, N), (1, 0, N)]
 SCALAR_COLS = 80
-GPSIMD_COLS = 416
-TILES = [(g, h) for h in range(M // P) for g in range(G)]
+GPSIMD_COLS_0 = 448
+GPSIMD_COLS_1 = 384
 
 
 def tile_rows_gglu_gelu_res_kernel(tc, x, w_words, w_scales, u_words, u_scales, r, out):
@@ -33,26 +36,32 @@ def tile_rows_gglu_gelu_res_kernel(tc, x, w_words, w_scales, u_words, u_scales, 
         ps = ctx.enter_context(tc.psum_pool(name="ps", bufs=1))
         ctx.enter_context(tc.manual_schedule())
 
-        words = [sb.tile([P, 2 * M], U8, name="words%d" % i, align_bytes=64) for i in range(2)]
-        scales = sb.tile([P, 2, M], U8, name="scales", align_bytes=64)
+        words = [sb.tile([P, 2 * M], U8, name="words%d" % i, align_bytes=64) for i in (W, U)]
+        scales = [sb.tile([P, M], U8, name="scales%d" % i, align_bytes=64) for i in (W, U)]
         x_codes = sb.tile([P, HALF + N], U32, name="x_codes", align_bytes=64)
         x_scales = sb.tile([P, HALF + N], U8, name="x_scales", align_bytes=64)
         x_bf = sb.tile([P, N, PACK], BF16, name="x_bf", align_bytes=64)
-        x_raw = [sb.tile([P, PACK, HALF], F32, name="x_raw%d" % i) for i in range(2)]
+        x_raw = [sb.tile([P, PACK, HALF], F32, name="x_raw%d" % (c * HALF)) for c in range(2)]
         zero = sb.tile([P, 1], F32, name="zero")
         bias = sb.tile([P, 1], F32, name="bias")
-        banks = [[ps.tile([P, N], F32, name="bank%d_%d" % (g, i)) for i in range(2)] for g in range(G)]
-        res = sb.tile([P, len(TILES), N], F32, name="res")
-        act = sb.tile([P, len(TILES), N], F32, name="act")
-        prod = sb.tile([P, len(TILES), N], F32, name="prod")
-        y = sb.tile([P, len(TILES), N], F32, name="y")
+        banks = [[ps.tile([P, N], F32, name="bank%d_%d" % (g, i)) for i in (W, U)] for g in range(G)]
+        total = G * N * M // P
+        res = sb.tile([P, total], F32, name="res")
+        act = sb.tile([P, total], F32, name="act")
+        prod = sb.tile([P, total], F32, name="prod")
+        y = sb.tile([P, total], F32, name="y")
 
-        nc.vector.memset(scales[:].rearrange("p i m -> p (i m)").bitcast(I32), 0)
+        def place(k, g):
+            widths = [hi - lo for m_tile, lo, hi in ROUNDS]
+            return G * sum(widths[:k]) + g * widths[k]
+
+        for i in (W, U):
+            nc.vector.memset(scales[i][:].bitcast(I32), 0)
+        nc.gpsimd.memset(zero[:], 0.0)
         nc.vector.memset(x_codes[:, 0:HALF], 0)
         nc.vector.memset(x_scales[:, 0:HALF].bitcast(I32), 0)
-        nc.gpsimd.memset(zero[:], 0.0)
 
-        x_view = x.rearrange("g (p j) n -> (g p) j n", j=PACK)
+        x_view = x.rearrange("g (p t) n -> (g p) t n", t=PACK)
 
         def load_x(c):
             nc.sync.dma_start(out=x_raw[c][:], in_=x_view[:, :, c * HALF : (c + 1) * HALF])
@@ -63,33 +72,42 @@ def tile_rows_gglu_gelu_res_kernel(tc, x, w_words, w_scales, u_words, u_scales, 
 
         def load_scales(queue, g, i):
             src = (w_scales, u_scales)[i][g]
-            queue.dma_start(out=scales[ROWS * g : ROWS * g + SCALE_ROWS, i, :].bitcast(I32), in_=src.bitcast(I32))
+            queue.dma_start(out=scales[i][ROWS * g : ROWS * g + SCALE_ROWS, :].bitcast(I32), in_=src.bitcast(I32))
 
-        def load_res(t, count, lo, hi):
-            g, h = TILES[t]
-            src = r[g : g + count, h * P : (h + 1) * P, lo:hi].rearrange("g p n -> p g n")
-            nc.sync.dma_start(out=res[:, t : t + count, lo:hi], in_=src)
+        def pieces(tile, k, g, count):
+            return tile[:, place(k, g) : place(k, g + count)].rearrange("p (g n) -> p g n", g=count)
+
+        def in_hbm(tensor, k, g, count):
+            m_tile, lo, hi = ROUNDS[k]
+            return tensor[g : g + count, m_tile * P : (m_tile + 1) * P, lo:hi].rearrange("g p n -> p g n")
+
+        def load_res(k, g, count):
+            nc.sync.dma_start(out=pieces(res, k, g, count), in_=in_hbm(r, k, g, count))
+
+        def store(k, g, count):
+            nc.sync.dma_start(out=in_hbm(out, k, g, count), in_=pieces(y, k, g, count))
 
         nc.scalar.activation(out=bias[:], in_=zero[:], func=GELU)
+
         load_x(0)
         for g in range(G):
-            load_scales(nc.sync, g, 0)
-        load_scales(nc.gpsimd, 0, 1)
-        load_words(0)
+            load_scales(nc.sync, g, W)
+        load_scales(nc.gpsimd, 0, U)
+        load_words(W)
         load_x(1)
-        load_words(1)
+        load_words(U)
         for g in range(1, G):
-            load_scales(nc.sync, g, 1)
-        load_res(0, 2, 0, HALF)
-        load_res(2, 2, 0, HALF)
-        load_res(0, G, HALF, N)
-        load_res(4, 2, 0, N)
-        load_res(6, 2, 0, N)
+            load_scales(nc.sync, g, U)
+        load_res(0, 0, 2)
+        load_res(0, 2, 2)
+        load_res(1, 0, G)
+        load_res(2, 0, 2)
+        load_res(2, 2, 2)
 
         def interleave(engine_copy, c, lo, hi):
             engine_copy(
-                out=x_bf[:, c * HALF + lo : c * HALF + hi, :].rearrange("p (c i) t -> p c t i", i=4),
-                in_=x_raw[c][:, :, lo:hi].rearrange("p t (c i) -> p c t i", i=4),
+                out=x_bf[:, c * HALF + lo : c * HALF + hi, :].rearrange("p (a i) t -> p a t i", i=RUN),
+                in_=x_raw[c][:, :, lo:hi].rearrange("p t (a i) -> p a t i", i=RUN),
             )
 
         def quantize(lo, hi):
@@ -106,75 +124,61 @@ def tile_rows_gglu_gelu_res_kernel(tc, x, w_words, w_scales, u_words, u_scales, 
             quantize(c * HALF, c * HALF + P)
             quantize(c * HALF + P, (c + 1) * HALF)
 
-        def product(t, i, first):
-            g, h = TILES[t]
+        def product(k, g, i):
+            m_tile, lo, hi = ROUNDS[k]
             rows = slice(ROWS * g, ROWS * (g + 1))
+            window = slice(HALF + hi - N, HALF + hi)
             nc.tensor.matmul_mx(
                 out=banks[g][i][:],
-                lhsT=words[i][rows, 2 * P * h : 2 * P * (h + 1)].bitcast(FP4X4),
-                lhsT_scale=scales[rows, i, P * h : P * (h + 1)],
-                rhs=x_codes[rows, first : first + N].bitcast(FP8X4),
-                rhs_scale=x_scales[rows, first : first + N],
+                lhsT=words[i][rows, 2 * P * m_tile : 2 * P * (m_tile + 1)].bitcast(FP4X4),
+                lhsT_scale=scales[i][rows, P * m_tile : P * (m_tile + 1)],
+                rhs=x_codes[rows, window].bitcast(FP8X4),
+                rhs_scale=x_scales[rows, window],
                 start=True,
                 stop=True,
             )
 
-        def gelu(t, lo, hi, at):
-            bank = banks[TILES[t][0]][0]
-            nc.scalar.activation(out=act[:, t, lo:hi], in_=bank[:, at : at + hi - lo], func=GELU, bias=bias[:])
+        def gate(k, g):
+            m_tile, lo, hi = ROUNDS[k]
+            used = slice(N - (hi - lo), N)
+            cols = slice(place(k, g), place(k, g + 1))
+            nc.scalar.activation(out=act[:, cols], in_=banks[g][W][:, used], func=GELU, bias=bias[:])
+            nc.vector.tensor_tensor(out=prod[:, cols], in0=banks[g][U][:, used], in1=act[:, cols], op=MULT)
+            if k + 1 < len(ROUNDS):
+                product(k + 1, g, W)
+                if g > 0:
+                    product(k + 1, g - 1, U)
+                if g == G - 1:
+                    product(k + 1, g, U)
 
-        def multiply(t, lo, hi, at):
-            bank = banks[TILES[t][0]][1]
-            nc.vector.tensor_tensor(out=prod[:, t, lo:hi], in0=bank[:, at : at + hi - lo], in1=act[:, t, lo:hi], op=MULT)
+        def add(engine, lo, hi):
+            engine.tensor_tensor(out=y[:, lo:hi], in0=prod[:, lo:hi], in1=res[:, lo:hi], op=ADD)
 
-        def gate(t, lo, hi):
-            gelu(t, lo, hi, N - (hi - lo))
-            multiply(t, lo, hi, N - (hi - lo))
-
-        def add(engine, t, count, lo, hi):
-            where = (slice(0, P), slice(t, t + count), slice(lo, hi))
-            engine.tensor_tensor(out=y[where], in0=prod[where], in1=res[where], op=ADD)
-
-        def store(t, count=1, lo=0, hi=N):
-            g, h = TILES[t]
-            dst = out[g : g + count, h * P : (h + 1) * P, lo:hi].rearrange("g p n -> p g n")
-            nc.sync.dma_start(out=dst, in_=y[:, t : t + count, lo:hi])
-
-        def refill(g, shift):
-            product(g + shift, 0, HALF)
-            if g > 0:
-                product(g - 1 + shift, 1, HALF)
-            if g == G - 1:
-                product(g + shift, 1, HALF)
-
-        for i in range(2):
+        for i in (W, U):
             for g in range(G):
-                product(g, i, 0)
+                product(0, g, i)
+
+        gate(0, 0)
+        add(nc.gpsimd, place(0, 0), place(0, 1))
+        for g in range(1, G):
+            gate(0, g)
+        add(nc.vector, place(0, 1), place(0, 2))
+        store(0, 0, 2)
+
+        add(nc.gpsimd, place(0, 2), place(0, 2) + GPSIMD_COLS_0)
         for g in range(G):
-            gate(g, 0, HALF)
-            refill(g, 0)
-            if g == 0:
-                add(nc.gpsimd, 0, 1, 0, HALF)
-        add(nc.vector, 1, 1, 0, HALF)
-        store(0, 2, 0, HALF)
-        add(nc.gpsimd, 2, 2, 0, HALF)
-        store(2, 2, 0, HALF)
-        for g in range(G):
-            gate(g, HALF, N)
-            refill(g, G)
-        add(nc.vector, 0, 2, HALF, N)
-        store(0, 2, HALF, N)
-        add(nc.gpsimd, 2, 2, HALF, N)
-        store(2, 2, HALF, N)
-        gate(4, 0, N)
-        gate(5, 0, N)
-        add(nc.vector, 4, 1, 0, N)
-        store(4)
-        add(nc.gpsimd, 5, 1, 0, GPSIMD_COLS)
-        gate(6, 0, N)
-        gate(7, 0, N)
-        add(nc.vector, 5, 1, GPSIMD_COLS, N)
-        store(5)
-        for t in (6, 7):
-            add(nc.vector, t, 1, 0, N)
-            store(t)
+            gate(1, g)
+        add(nc.vector, place(0, 2) + GPSIMD_COLS_0, place(2, 0) - GPSIMD_COLS_1)
+        store(0, 2, 2)
+        store(1, 0, 2)
+
+        add(nc.gpsimd, place(2, 0) - GPSIMD_COLS_1, place(2, 0))
+        store(1, 2, 2)
+        gate(2, 0)
+        add(nc.gpsimd, place(2, 0), place(2, 1))
+        store(2, 0, 1)
+        for g in range(1, G):
+            gate(2, g)
+        for g in range(1, G):
+            add(nc.vector, place(2, g), place(2, g + 1))
+            store(2, g, 1)

@@ -25,8 +25,6 @@ RUN = 4
 W, U = 0, 1
 ROUNDS = [(0, 0, HALF), (0, HALF, N), (1, 0, N)]
 SCALAR_COLS = 80
-GPSIMD_COLS_0 = 448
-GPSIMD_COLS_1 = 384
 
 
 def tile_rows_gglu_gelu_res_kernel(tc, x, w_words, w_scales, u_words, u_scales, r, out):
@@ -165,20 +163,24 @@ def tile_rows_gglu_gelu_res_kernel(tc, x, w_words, w_scales, u_words, u_scales, 
         add(nc.vector, place(0, 1), place(0, 2))
         store(0, 0, 2)
 
-        add(nc.gpsimd, place(0, 2), place(0, 2) + GPSIMD_COLS_0)
+        add(nc.gpsimd, place(0, 2), place(1, 0))
+        store(0, 2, 2)
         for g in range(G):
             gate(1, g)
-        add(nc.vector, place(0, 2) + GPSIMD_COLS_0, place(2, 0) - GPSIMD_COLS_1)
-        store(0, 2, 2)
+        add(nc.vector, place(1, 0), place(1, 2))
         store(1, 0, 2)
 
-        add(nc.gpsimd, place(2, 0) - GPSIMD_COLS_1, place(2, 0))
+        add(nc.gpsimd, place(1, 2), place(2, 0))
         store(1, 2, 2)
         gate(2, 0)
-        add(nc.gpsimd, place(2, 0), place(2, 1))
+        gate(2, 1)
+        add(nc.vector, place(2, 0), place(2, 1))
         store(2, 0, 1)
-        for g in range(1, G):
-            gate(2, g)
-        for g in range(1, G):
+
+        add(nc.gpsimd, place(2, 1), place(2, 2))
+        store(2, 1, 1)
+        gate(2, 2)
+        gate(2, 3)
+        for g in (2, 3):
             add(nc.vector, place(2, g), place(2, g + 1))
             store(2, g, 1)

@@ -25,6 +25,8 @@ RUN = 4
 W, U = 0, 1
 ROUNDS = [(0, 0, HALF), (0, HALF, N), (1, 0, N)]
 SCALAR_COLS = 80
+GPSIMD_COLS_FIRST = 192
+GPSIMD_COLS = 480
 
 
 def tile_rows_gglu_gelu_res_kernel(tc, x, w_words, w_scales, u_words, u_scales, r, out):
@@ -157,20 +159,20 @@ def tile_rows_gglu_gelu_res_kernel(tc, x, w_words, w_scales, u_words, u_scales, 
                 product(0, g, i)
 
         gate(0, 0)
-        add(nc.gpsimd, place(0, 0), place(0, 1))
+        add(nc.gpsimd, place(0, 0), GPSIMD_COLS_FIRST)
         for g in range(1, G):
             gate(0, g)
-        add(nc.vector, place(0, 1), place(0, 2))
+        add(nc.vector, GPSIMD_COLS_FIRST, place(0, 2))
         store(0, 0, 2)
 
-        add(nc.gpsimd, place(0, 2), place(1, 0))
-        store(0, 2, 2)
+        add(nc.gpsimd, place(0, 2), place(0, 2) + GPSIMD_COLS)
         for g in range(G):
             gate(1, g)
-        add(nc.vector, place(1, 0), place(1, 2))
+        add(nc.vector, place(0, 2) + GPSIMD_COLS, place(2, 0) - GPSIMD_COLS)
+        store(0, 2, 2)
         store(1, 0, 2)
 
-        add(nc.gpsimd, place(1, 2), place(2, 0))
+        add(nc.gpsimd, place(2, 0) - GPSIMD_COLS, place(2, 0))
         store(1, 2, 2)
         gate(2, 0)
         gate(2, 1)

@@ -22,6 +22,7 @@ ROWS = D // PACK
 SCALE_ROWS = D // 32
 HALF = N // 2
 RUN = 4
+ALIGN = 256
 W, U = 0, 1
 ROUNDS = [(0, 0, HALF), (0, HALF, N), (1, 0, N)]
 SCALAR_COLS = 80
@@ -36,20 +37,20 @@ def tile_rows_gglu_gelu_res_kernel(tc, x, w_words, w_scales, u_words, u_scales, 
         ps = ctx.enter_context(tc.psum_pool(name="ps", bufs=1))
         ctx.enter_context(tc.manual_schedule())
 
-        words = [sb.tile([P, 2 * M], U8, name="words%d" % i, align_bytes=64) for i in (W, U)]
-        scales = [sb.tile([P, M], U8, name="scales%d" % i, align_bytes=64) for i in (W, U)]
-        x_codes = sb.tile([P, HALF + N], U32, name="x_codes", align_bytes=64)
-        x_scales = sb.tile([P, HALF + N], U8, name="x_scales", align_bytes=64)
-        x_bf = sb.tile([P, N, PACK], BF16, name="x_bf", align_bytes=64)
-        x_raw = [sb.tile([P, PACK, HALF], F32, name="x_raw%d" % (c * HALF)) for c in range(2)]
+        words = [sb.tile([P, 2 * M], U8, name="words%d" % i, align_bytes=ALIGN) for i in (W, U)]
+        scales = [sb.tile([P, M], U8, name="scales%d" % i, align_bytes=ALIGN) for i in (W, U)]
+        x_codes = sb.tile([P, HALF + N], U32, name="x_codes", align_bytes=ALIGN)
+        x_scales = sb.tile([P, HALF + N], U8, name="x_scales", align_bytes=ALIGN)
+        x_bf = sb.tile([P, N, PACK], BF16, name="x_bf", align_bytes=ALIGN)
+        x_raw = [sb.tile([P, PACK, HALF], F32, name="x_raw%d" % (c * HALF), align_bytes=ALIGN) for c in range(2)]
         zero = sb.tile([P, 1], F32, name="zero")
         bias = sb.tile([P, 1], F32, name="bias")
         banks = [[ps.tile([P, N], F32, name="bank%d_%d" % (g, i)) for i in (W, U)] for g in range(G)]
         total = G * N * M // P
-        res = sb.tile([P, total], F32, name="res")
-        act = sb.tile([P, total], F32, name="act")
-        prod = sb.tile([P, total], F32, name="prod")
-        y = sb.tile([P, total], F32, name="y")
+        res = sb.tile([P, total], F32, name="res", align_bytes=ALIGN)
+        act = sb.tile([P, total], F32, name="act", align_bytes=ALIGN)
+        prod = sb.tile([P, total], F32, name="prod", align_bytes=ALIGN)
+        y = sb.tile([P, total], F32, name="y", align_bytes=ALIGN)
 
         def place(k, g):
             widths = [hi - lo for m_tile, lo, hi in ROUNDS]

@@ -22,7 +22,7 @@ ROWS = D // PACK
 SCALE_ROWS = D // 32
 HALF = N // 2
 RUN = 4
-ALIGN = 256
+ALIGN = 2048
 W, U = 0, 1
 ROUNDS = [(0, 0, HALF), (0, HALF, N), (1, 0, N)]
 SCALAR_COLS = 80

@@ -91,11 +91,13 @@ def tile_rows_gglu_gelu_res_kernel(tc, x, w_words, w_scales, u_words, u_scales, 
         nc.scalar.activation(out=bias[:], in_=zero[:], func=GELU)
 
         load_x(0)
-        for g in range(G):
+        load_words(W)
+        for g in (0, 1):
             load_scales(nc.sync, g, W)
         load_scales(nc.gpsimd, 0, U)
-        load_words(W)
         load_x(1)
+        for g in (2, 3):
+            load_scales(nc.sync, g, W)
         load_words(U)
         for g in range(1, G):
             load_scales(nc.sync, g, U)

@@ -171,11 +171,11 @@ def tile_rows_gglu_gelu_res_kernel(tc, x, w_words, w_scales, u_words, u_scales, 
         add(nc.gpsimd, place(0, 2), place(0, 2) + GPSIMD_COLS)
         for g in range(G):
             gate(1, g)
-        add(nc.vector, place(0, 2) + GPSIMD_COLS, place(2, 0) - GPSIMD_COLS)
+        add(nc.vector, place(0, 2) + GPSIMD_COLS, place(1, 2))
         store(0, 2, 2)
         store(1, 0, 2)
 
-        add(nc.gpsimd, place(2, 0) - GPSIMD_COLS, place(2, 0))
+        add(nc.gpsimd, place(1, 2), place(2, 0))
         store(1, 2, 2)
         gate(2, 0)
         gate(2, 1)

@@ -94,14 +94,15 @@ def tile_rows_gglu_gelu_res_kernel(tc, x, w_words, w_scales, u_words, u_scales, 
         load_words(W)
         for g in (0, 1):
             load_scales(nc.sync, g, W)
-        load_scales(nc.gpsimd, 0, U)
+            load_scales(nc.gpsimd, g, U)
         load_x(1)
         for g in (2, 3):
             load_scales(nc.sync, g, W)
         load_words(U)
-        for g in range(1, G):
+        for g in (2, 3):
             load_scales(nc.sync, g, U)
-        load_res(0, 0, 2)
+        load_res(0, 0, 1)
+        load_res(0, 1, 1)
         load_res(0, 2, 2)
         load_res(1, 0, G)
         load_res(2, 0, 2)

@@ -93,11 +93,11 @@ def tile_rows_gglu_gelu_res_kernel(tc, x, w_words, w_scales, u_words, u_scales, 
         load_x(0)
         load_words(W)
         for g in (0, 1):
-            load_scales(nc.sync, g, W)
             load_scales(nc.gpsimd, g, U)
-        load_x(1)
-        for g in (2, 3):
+        for g in range(G - 1):
             load_scales(nc.sync, g, W)
+        load_x(1)
+        load_scales(nc.sync, G - 1, W)
         load_words(U)
         for g in (2, 3):
             load_scales(nc.sync, g, U)

from contextlib import ExitStack

import concourse.mybir as mybir

G, D, M, N = 4, 128, 256, 512
FLOPS = 2 * 2 * G * D * M * N

F32 = mybir.dt.float32
BF16 = mybir.dt.bfloat16
U32 = mybir.dt.uint32
I32 = mybir.dt.int32
U8 = mybir.dt.uint8
FP8X4 = mybir.dt.float8_e4m3fn_x4
FP4X4 = mybir.dt.float4_e2m1fn_x4
GELU = mybir.ActivationFunctionType.Gelu_apprx_tanh
ADD = mybir.AluOpType.add
MULT = mybir.AluOpType.mult

P = 128
PACK = 4
ROWS = D // PACK
SCALE_ROWS = D // 32
HALF = N // 2
RUN = 4
ALIGN = 2048
W, U = 0, 1
ROUNDS = [(0, 0, HALF), (0, HALF, N), (1, 0, N)]
SCALAR_COLS = 80
GPSIMD_COLS_FIRST = 192
GPSIMD_COLS = 480


def tile_rows_gglu_gelu_res_kernel(tc, x, w_words, w_scales, u_words, u_scales, r, out):
    nc = tc.nc
    with ExitStack() as ctx:
        sb = ctx.enter_context(tc.tile_pool(name="sb", bufs=1))
        ps = ctx.enter_context(tc.psum_pool(name="ps", bufs=1))
        ctx.enter_context(tc.manual_schedule())

        words = [sb.tile([P, 2 * M], U8, name="words%d" % i, align_bytes=ALIGN) for i in (W, U)]
        scales = [sb.tile([P, M], U8, name="scales%d" % i, align_bytes=ALIGN) for i in (W, U)]
        x_codes = sb.tile([P, HALF + N], U32, name="x_codes", align_bytes=ALIGN)
        x_scales = sb.tile([P, HALF + N], U8, name="x_scales", align_bytes=ALIGN)
        x_bf = sb.tile([P, N, PACK], BF16, name="x_bf", align_bytes=ALIGN)
        x_raw = [sb.tile([P, PACK, HALF], F32, name="x_raw%d" % (c * HALF), align_bytes=ALIGN) for c in range(2)]
        zero = sb.tile([P, 1], F32, name="zero")
        bias = sb.tile([P, 1], F32, name="bias")
        banks = [[ps.tile([P, N], F32, name="bank%d_%d" % (g, i)) for i in (W, U)] for g in range(G)]
        total = G * N * M // P
        res = sb.tile([P, total], F32, name="res", align_bytes=ALIGN)
        act = sb.tile([P, total], F32, name="act", align_bytes=ALIGN)
        prod = sb.tile([P, total], F32, name="prod", align_bytes=ALIGN)
        y = sb.tile([P, total], F32, name="y", align_bytes=ALIGN)

        def place(k, g):
            widths = [hi - lo for m_tile, lo, hi in ROUNDS]
            return G * sum(widths[:k]) + g * widths[k]

        for i in (W, U):
            nc.vector.memset(scales[i][:].bitcast(I32), 0)
        nc.gpsimd.memset(zero[:], 0.0)
        nc.vector.memset(x_codes[:, 0:HALF], 0)
        nc.vector.memset(x_scales[:, 0:HALF].bitcast(I32), 0)

        x_view = x.rearrange("g (p t) n -> (g p) t n", t=PACK)

        def load_x(c):
            nc.sync.dma_start(out=x_raw[c][:], in_=x_view[:, :, c * HALF : (c + 1) * HALF])

        def load_words(i):
            src = (w_words, u_words)[i].rearrange("g p b -> (g p) b")
            nc.sync.dma_start(out=words[i][:].bitcast(I32), in_=src.bitcast(I32))

        def load_scales(queue, g, i):
            src = (w_scales, u_scales)[i][g]
            queue.dma_start(out=scales[i][ROWS * g : ROWS * g + SCALE_ROWS, :].bitcast(I32), in_=src.bitcast(I32))

        def pieces(tile, k, g, count):
            return tile[:, place(k, g) : place(k, g + count)].rearrange("p (g n) -> p g n", g=count)

        def in_hbm(tensor, k, g, count):
            m_tile, lo, hi = ROUNDS[k]
            return tensor[g : g + count, m_tile * P : (m_tile + 1) * P, lo:hi].rearrange("g p n -> p g n")

        def load_res(k, g, count):
            nc.sync.dma_start(out=pieces(res, k, g, count), in_=in_hbm(r, k, g, count))

        def store(k, g, count):
            nc.sync.dma_start(out=in_hbm(out, k, g, count), in_=pieces(y, k, g, count))

        nc.scalar.activation(out=bias[:], in_=zero[:], func=GELU)

        load_x(0)
        load_words(W)
        for g in (0, 1):
            load_scales(nc.gpsimd, g, U)
        for g in range(G - 1):
            load_scales(nc.sync, g, W)
        load_x(1)
        load_scales(nc.sync, G - 1, W)
        load_words(U)
        for g in (2, 3):
            load_scales(nc.sync, g, U)
        load_res(0, 0, 1)
        load_res(0, 1, 1)
        load_res(0, 2, 2)
        load_res(1, 0, G)
        load_res(2, 0, 2)
        load_res(2, 2, 2)

        def interleave(engine_copy, c, lo, hi):
            engine_copy(
                out=x_bf[:, c * HALF + lo : c * HALF + hi, :].rearrange("p (a i) t -> p a t i", i=RUN),
                in_=x_raw[c][:, :, lo:hi].rearrange("p t (a i) -> p a t i", i=RUN),
            )

        def quantize(lo, hi):
            nc.vector.quantize_mx(
                out=x_codes[:, HALF + lo : HALF + hi].bitcast(FP8X4),
                scales=x_scales[:, HALF + lo : HALF + hi],
                in_=x_bf[:, lo:hi, :].rearrange("p c t -> p (c t)"),
            )

        for c in range(2):
            interleave(nc.vector.tensor_copy, c, 0, P)
            interleave(nc.vector.tensor_copy, c, P, HALF - SCALAR_COLS)
            interleave(nc.scalar.copy, c, HALF - SCALAR_COLS, HALF)
            quantize(c * HALF, c * HALF + P)
            quantize(c * HALF + P, (c + 1) * HALF)

        def product(k, g, i):
            m_tile, lo, hi = ROUNDS[k]
            rows = slice(ROWS * g, ROWS * (g + 1))
            window = slice(HALF + hi - N, HALF + hi)
            nc.tensor.matmul_mx(
                out=banks[g][i][:],
                lhsT=words[i][rows, 2 * P * m_tile : 2 * P * (m_tile + 1)].bitcast(FP4X4),
                lhsT_scale=scales[i][rows, P * m_tile : P * (m_tile + 1)],
                rhs=x_codes[rows, window].bitcast(FP8X4),
                rhs_scale=x_scales[rows, window],
                start=True,
                stop=True,
            )

        def gate(k, g):
            m_tile, lo, hi = ROUNDS[k]
            used = slice(N - (hi - lo), N)
            cols = slice(place(k, g), place(k, g + 1))
            nc.scalar.activation(out=act[:, cols], in_=banks[g][W][:, used], func=GELU, bias=bias[:])
            nc.vector.tensor_tensor(out=prod[:, cols], in0=banks[g][U][:, used], in1=act[:, cols], op=MULT)
            if k + 1 < len(ROUNDS):
                product(k + 1, g, W)
                if g > 0:
                    product(k + 1, g - 1, U)
                if g == G - 1:
                    product(k + 1, g, U)

        def add(engine, lo, hi):
            engine.tensor_tensor(out=y[:, lo:hi], in0=prod[:, lo:hi], in1=res[:, lo:hi], op=ADD)

        for i in (W, U):
            for g in range(G):
                product(0, g, i)

        gate(0, 0)
        add(nc.gpsimd, place(0, 0), GPSIMD_COLS_FIRST)
        for g in range(1, G):
            gate(0, g)
        add(nc.vector, GPSIMD_COLS_FIRST, place(0, 2))
        store(0, 0, 2)

        add(nc.gpsimd, place(0, 2), place(0, 2) + GPSIMD_COLS)
        for g in range(G):
            gate(1, g)
        add(nc.vector, place(0, 2) + GPSIMD_COLS, place(1, 2))
        store(0, 2, 2)
        store(1, 0, 2)

        add(nc.gpsimd, place(1, 2), place(2, 0))
        store(1, 2, 2)
        gate(2, 0)
        gate(2, 1)
        add(nc.vector, place(2, 0), place(2, 1))
        store(2, 0, 1)

        add(nc.gpsimd, place(2, 1), place(2, 2))
        store(2, 1, 1)
        gate(2, 2)
        gate(2, 3)
        for g in (2, 3):
            add(nc.vector, place(2, g), place(2, g + 1))
            store(2, g, 1)
